import numpy as np, ml_dtypes
CORES = [9,17,57,81,121,137,145,185,209,249]
N = 10
F = 512
GROUPS = [[0,1,2,3,4],[5,6,7,8,9]]
def setup_inputs(rng):
    return {"x": rng.standard_normal((N, 128, F), dtype=np.float32).astype(ml_dtypes.bfloat16), "w": (rng.standard_normal((N, 128, 128), dtype=np.float32) / 11).astype(ml_dtypes.bfloat16)}
def setup_inputs_big(rng):
    d = setup_inputs(rng)
    for k in ("x", "w"): d[k] = (d[k].astype(np.float32) * 1024.0).astype(d[k].dtype)
    return d
def setup_inputs_small(rng):
    d = setup_inputs(rng)
    for k in ("x", "w"): d[k] = (d[k].astype(np.float32) * (1 / 1024.0)).astype(d[k].dtype)
    return d
def setup_inputs_apart(rng):
    d = setup_inputs(rng)
    f = (10.0 ** rng.permutation(np.linspace(-1.5, 1.5, N))).astype(np.float32).reshape(N, 1, 1)
    for k in ("x", "w"): d[k] = (d[k].astype(np.float32) * f).astype(d[k].dtype)
    return d
def reference(x, w):
    X, W = x.astype(np.float64), w.astype(np.float64)
    s = sum(W[g[0]].T @ np.maximum(sum(X[j] for j in g), 0.0) for g in GROUPS).astype(ml_dtypes.bfloat16)
    return {"y": np.broadcast_to(s, (N,) + s.shape)}

@@ -1,0 +1,260 @@
+import comms_topo
+from concourse.bass import DstId, RemoteDMATransfer
+from concourse.mybir import dt, AluOpType
+
+Q = 4
+CW = 128
+
+SCRATCH = {
+    "xs": ("sbuf", [128, 512], "bfloat16"),
+    "xin": ("sbuf", [128, 10 * CW], "bfloat16"),
+    "hx": ("sbuf", [128, CW], "bfloat16"),
+    "wd": ("dram", [128, 128], "bfloat16"),
+    "wb": ("sbuf", [128, 2 * 128], "bfloat16"),
+    "ybuf": ("sbuf", [128, 512], "bfloat16"),
+    "ida": ("sbuf", [128, 129], "bfloat16"),
+    "idd": ("dram", [129, 128], "bfloat16"),
+    "idn": ("sbuf", [128, 128], "bfloat16"),
+    "zero": ("sbuf", [128, CW], "float32"),
+    "t0": ("sbuf", [128, CW], "bfloat16"),
+    "t1": ("sbuf", [128, CW], "bfloat16"),
+    "ps0": ("psum", [128, 512], "float32"),
+    "ps1": ("psum", [128, 512], "float32"),
+    "psy": ("psum", [128, 512], "float32"),
+}
+SEMAPHORES = ["xl", "wl", "hw", "hxs", "xd", "xc", "wa", "ya", "ls", "fill", "id1", "id2",
+              "sm0", "sm1", "ts0", "ts1", "ys", "yc", "st"]
+
+
+def _bits(mask):
+    return [b for b in range(mask.bit_length()) if (mask >> b) & 1]
+
+
+def _m(bits):
+    return sum(1 << b for b in bits)
+
+
+def _split(bits, n):
+    p = 1
+    while p * 2 * n <= len(bits):
+        p *= 2
+    sizes = [p] * n
+    left = len(bits) - p * n
+    for i in range(n):
+        if left >= sizes[i]:
+            left -= sizes[i]
+            sizes[i] *= 2
+    out, o = [], 0
+    for s in sizes:
+        out.append(bits[o:o + s])
+        o += s
+    return out
+
+
+def _plan(T, topo):
+    cores = list(T.cores)
+    n = len(cores)
+    groups = T.tables["GROUPS"]
+    wsrc = [grp[0] for grp in groups]
+    planes = []
+    for r in range(n):
+        for p in planes:
+            if topo.same_plane(cores[r], cores[p[0]]):
+                p.append(r)
+                break
+        else:
+            planes.append([r])
+    plane_of = {}
+    for i, p in enumerate(planes):
+        for r in p:
+            plane_of[r] = i
+    owners = [[r for r in p if r not in wsrc][:Q] for p in planes]
+    hosts = 1 + max(topo.host(c) for c in cores)
+    ports = {}
+    for r in range(n):
+        rc = cores[r]
+        far = cores[planes[1 - plane_of[r]][0]]
+        can = [c for c in range(hosts * topo.CORES_PER_HOST)
+               if c != rc and topo.host(c) == topo.host(rc) and topo.chip(c) == topo.chip(rc) and topo.may_write(c, far)]
+        near = [c for c in can if topo.die(c) == topo.die(rc)]
+        away = [c for c in can if topo.die(c) != topo.die(rc)]
+        order = []
+        for a, b in zip(near, away):
+            order += [a, b]
+        ports[r] = order[:Q]
+    return {"cores": cores, "n": n, "groups": groups, "wsrc": wsrc, "planes": planes, "plane_of": plane_of,
+            "owners": owners, "ports": ports}
+
+
+def _port(P, r, k):
+    return P["ports"][r][(k + P["planes"][P["plane_of"][r]].index(r)) % Q]
+
+
+def _direct(P, topo, r):
+    own = P["owners"][P["plane_of"][r]]
+    todo = [(k, o) for k, o in enumerate(own) if o != r]
+    src = P["cores"][r]
+    bits = _bits(topo.mask(src, P["cores"][todo[0][1]]))
+    return [(k, o, e) for (k, o), e in zip(todo, _split(bits, len(todo)))]
+
+
+def _dst(topo, d, src):
+    rid, pid = topo.addr(d, src)
+    return DstId(rid=rid, pnc=pid)
+
+
+def _common(topo, src, dests):
+    m = topo.mask(src, dests[0])
+    for d in dests[1:]:
+        m &= topo.mask(src, d)
+    return m
+
+
+def _col(k):
+    return slice(k * CW, (k + 1) * CW)
+
+
+def _helper(g, core, T, topo, P, r):
+    cores = P["cores"]
+    k = [q for q in range(Q) if _port(P, r, q) == core][0]
+    pl = P["plane_of"][r]
+    far, near = cores[P["owners"][1 - pl][k]], cores[P["owners"][pl][k]]
+    sent = 0
+    if r in P["wsrc"]:
+        gi = P["wsrc"].index(r)
+        dests = [far, near]
+        m = _common(topo, core, dests)
+        g.wait_ge(T.sem.hw, len(_bits(_common(topo, cores[r], P["ports"][r]))))
+        g.remote_dma_fused([RemoteDMATransfer(
+            dst_ids=[_dst(topo, d, core) for d in dests], dma_engine_mask=m, remote_sem=T.sem.wa,
+            srcs=[T.wd[:, :]], dsts=[T.wb[:, gi * 128:(gi + 1) * 128] for d in dests], alu_op=0)], local_sem=T.sem.ls)
+        sent += len(_bits(m))
+    g.wait_ge(T.sem.hxs, len(_split(_bits(_common(topo, cores[r], P["ports"][r])), Q)[k]))
+    m = topo.mask(core, far)
+    rid, pid = topo.addr(far, core)
+    g.remote_dma(out_ap=T.xin[:, _col(r)], in_ap=T.hx[:, :], remote_sem=T.sem.xc, local_sem=T.sem.ls,
+                 pid=pid, routing_id=rid, dma_engine_mask=m)
+    sent += len(_bits(m))
+    g.wait_ge(T.sem.ls, sent)
+
+
+def rank_program(g, core, T, topo):
+    P = _plan(T, topo)
+    cores, n = P["cores"], P["n"]
+    rank = T.rank_of(core)
+    if rank is None:
+        for r in range(n):
+            if core in P["ports"][r]:
+                _helper(g, core, T, topo, P, r)
+        return
+
+    pl = P["plane_of"][rank]
+    plane = P["planes"][pl]
+    own = P["owners"][pl]
+    is_owner = rank in own
+    sent = 0
+
+    g.sync.dma_start(T.xs[:, :], T.x[:, :]).then_inc(T.sem.xl, 16)
+    if rank in P["wsrc"]:
+        g.scalar.dma_start(T.wd[:, :], T.w[:, :]).then_inc(T.sem.wl, 16)
+    if is_owner:
+        g.vector.memset(T.ida[:, 0:1], 1.0).then_inc(T.sem.fill, 1)
+        g.vector.memset(T.ida[:, 1:129], 0.0).then_inc(T.sem.fill, 1)
+        g.vector.memset(T.zero[:, :], 0.0).then_inc(T.sem.fill, 1)
+        g.scalar.wait_ge(T.sem.fill, 3)
+        g.scalar.dma_start(T.idd[:, :], T.ida[:, :]).then_inc(T.sem.id1, 16)
+        g.scalar.wait_ge(T.sem.id1, 16)
+        g.scalar.dma_start(T.idn[:, :], T.idd[0:128, :]).then_inc(T.sem.id2, 16)
+
+    pc = P["ports"][rank]
+    chipmask = _common(topo, core, pc)
+    if rank in P["wsrc"]:
+        g.wait_ge(T.sem.wl, 16)
+        g.remote_dma_fused([RemoteDMATransfer(
+            dst_ids=[_dst(topo, c, core) for c in pc], dma_engine_mask=chipmask, remote_sem=T.sem.hw,
+            srcs=[T.wd[:, :]], dsts=[T.wd[:, :] for c in pc], alu_op=0)], local_sem=T.sem.ls)
+        sent += len(_bits(chipmask))
+
+    g.wait_ge(T.sem.xl, 16)
+    eng = _split(_bits(chipmask), Q)
+    g.remote_dma_fused([RemoteDMATransfer(
+        dst_ids=[_dst(topo, _port(P, rank, k), core)], dma_engine_mask=_m(eng[k]), remote_sem=T.sem.hxs,
+        src=T.xs[:, _col(k)], dst=T.hx[:, :]) for k in range(Q)], local_sem=T.sem.ls)
+    sent += sum(len(e) for e in eng)
+    dr = _direct(P, topo, rank)
+    g.remote_dma_fused([RemoteDMATransfer(
+        dst_ids=[_dst(topo, cores[o], core)], dma_engine_mask=_m(e), remote_sem=T.sem.xd,
+        src=T.xs[:, _col(k)], dst=T.xin[:, _col(rank)]) for k, o, e in dr], local_sem=T.sem.ls)
+    sent += sum(len(e) for k, o, e in dr)
+
+    n_y = 0
+    for o in own:
+        if o != rank:
+            n_y += len(_bits(_common(topo, cores[o], [cores[d] for d in plane if d != o])))
+
+    if is_owner:
+        k = own.index(rank)
+        n_xd = sum(len(e) for j in plane if j != rank for q, o, e in _direct(P, topo, j) if o == rank)
+        far = [j for j in range(n) if P["plane_of"][j] != pl]
+        n_xc = sum(len(_bits(topo.mask(_port(P, j, k), core))) for j in far)
+        n_wa = sum(len(_bits(_common(topo, _port(P, j, k), [core]))) for j in P["wsrc"])
+        ps = [T.ps0, T.ps1]
+        tt = [T.t0, T.t1]
+        sm = [T.sem.sm0, T.sem.sm1]
+        ts = [T.sem.ts0, T.sem.ts1]
+        te, ve = g.tensor, g.vector
+
+        def add(gi, j):
+            seq = _order(P, gi, rank)
+            rhs = T.xs[:, _col(k)] if j == rank else T.xin[:, _col(j)]
+            ins = te.matmul(ps[gi][:, 0:CW], T.idn[:, :], rhs, j == seq[0], j == seq[-1])
+            if j == seq[-1]:
+                ins.then_inc(sm[gi], 1)
+
+        te.wait_ge(T.sem.id2, 16)
+        te.wait_ge(T.sem.xl, 16)
+        for gi, grp in enumerate(P["groups"]):
+            if rank in grp:
+                add(gi, rank)
+        te.wait_ge(T.sem.xd, n_xd)
+        for gi, grp in enumerate(P["groups"]):
+            for j in _order(P, gi, rank):
+                if j != rank and P["plane_of"][j] == pl:
+                    add(gi, j)
+        te.wait_ge(T.sem.xc, n_xc)
+        for gi, grp in enumerate(P["groups"]):
+            for j in _order(P, gi, rank):
+                if P["plane_of"][j] != pl:
+                    add(gi, j)
+        ve.wait_ge(T.sem.fill, 3)
+        for gi in range(len(ps)):
+            ve.wait_ge(sm[gi], 1)
+            ve.tensor_tensor(tt[gi][:, :], ps[gi][:, 0:CW], T.zero[:, :], AluOpType.max).then_inc(ts[gi], 1)
+        te.wait_ge(T.sem.wa, n_wa)
+        for gi in range(len(ps)):
+            te.wait_ge(ts[gi], 1)
+            ins = te.matmul(T.psy[:, 0:CW], T.wb[:, gi * 128:(gi + 1) * 128], tt[gi][:, :], gi == 0, gi == len(ps) - 1)
+        ins.then_inc(T.sem.ys, 1)
+        ve.wait_ge(T.sem.ys, 1)
+        ve.tensor_copy(T.ybuf[:, _col(k)], T.psy[:, 0:CW]).then_inc(T.sem.yc, 1)
+
+        dests = [cores[d] for d in plane if d != rank]
+        m = _common(topo, core, dests)
+        g.wait_ge(T.sem.yc, 1)
+        g.remote_dma_fused([RemoteDMATransfer(
+            dst_ids=[_dst(topo, d, core) for d in dests], dma_engine_mask=m, remote_sem=T.sem.ya,
+            srcs=[T.ybuf[:, _col(k)]], dsts=[T.ybuf[:, _col(k)] for d in dests], alu_op=0)], local_sem=T.sem.ls)
+        sent += len(_bits(m))
+        g.sync.wait_ge(T.sem.yc, 1)
+
+    g.sync.wait_ge(T.sem.ya, n_y)
+    g.sync.dma_start(T.y[:, :], T.ybuf[:, :]).then_inc(T.sem.st, 16)
+    g.sync.wait_ge(T.sem.st, 16)
+    g.wait_ge(T.sem.ls, sent)
+
+
+def _order(P, gi, rank):
+    pl = P["plane_of"][rank]
+    grp = P["groups"][gi]
+    return ([j for j in grp if j == rank] + [j for j in grp if j != rank and P["plane_of"][j] == pl]
+            + [j for j in grp if P["plane_of"][j] != pl])

@@ -1,19 +1,22 @@
 import comms_topo
 from concourse.bass import DstId, RemoteDMATransfer
-from concourse.mybir import dt, AluOpType
+from concourse.mybir import dt, AluOpType, ActivationFunctionType
 
 Q = 4
 CW = 128
+H = 2
+QH = Q // H
 
 SCRATCH = {
     "xs": ("sbuf", [128, 512], "bfloat16"),
     "xin": ("sbuf", [128, 10 * CW], "bfloat16"),
-    "hx": ("sbuf", [128, CW], "bfloat16"),
+    "hx": ("sbuf", [128, QH * CW], "bfloat16"),
+    "hy": ("sbuf", [128, CW], "bfloat16"),
     "wd": ("dram", [128, 128], "bfloat16"),
     "wb": ("sbuf", [128, 2 * 128], "bfloat16"),
     "ybuf": ("sbuf", [128, 512], "bfloat16"),
-    "ida": ("sbuf", [128, 129], "bfloat16"),
-    "idd": ("dram", [129, 128], "bfloat16"),
+    "one": ("sbuf", [128, 128], "bfloat16"),
+    "ib": ("sbuf", [128, 128], "bfloat16"),
     "idn": ("sbuf", [128, 128], "bfloat16"),
     "zero": ("sbuf", [128, CW], "float32"),
     "t0": ("sbuf", [128, CW], "bfloat16"),
@@ -22,8 +25,8 @@ SCRATCH = {
     "ps1": ("psum", [128, 512], "float32"),
     "psy": ("psum", [128, 512], "float32"),
 }
-SEMAPHORES = ["xl", "wl", "hw", "hxs", "xd", "xc", "wa", "ya", "ls", "fill", "id1", "id2",
-              "sm0", "sm1", "ts0", "ts1", "ys", "yc", "st"]
+SEMAPHORES = ["xl", "wl", "hw", "hxs", "wa", "ya", "yh", "ls", "fill", "fz", "idb", "ida",
+              "sm0", "sm1", "ts0", "ts1", "ys", "yc", "st"] + ["xa%d" % j for j in range(10)]
 
 
 def _bits(mask):
@@ -81,13 +84,21 @@ def _plan(T, topo):
         order = []
         for a, b in zip(near, away):
             order += [a, b]
-        ports[r] = order[:Q]
+        ports[r] = order[:2 * H]
     return {"cores": cores, "n": n, "groups": groups, "wsrc": wsrc, "planes": planes, "plane_of": plane_of,
             "owners": owners, "ports": ports}
 
 
-def _port(P, r, k):
-    return P["ports"][r][(k + P["planes"][P["plane_of"][r]].index(r)) % Q]
+def _xport(P, r, h):
+    return P["ports"][r][(h + P["planes"][P["plane_of"][r]].index(r)) % H]
+
+
+def _wport(P, r, h):
+    return P["ports"][r][H + (h + P["wsrc"].index(r)) % H]
+
+
+def _pair(P, pl, h):
+    return [P["cores"][P["owners"][pl][h * QH + i]] for i in range(QH)]
 
 
 def _direct(P, topo, r):
@@ -96,6 +107,54 @@ def _direct(P, topo, r):
     src = P["cores"][r]
     bits = _bits(topo.mask(src, P["cores"][todo[0][1]]))
     return [(k, o, e) for (k, o), e in zip(todo, _split(bits, len(todo)))]
+
+
+def _cross(P, topo, r, h):
+    fo = _pair(P, 1 - P["plane_of"][r], h)
+    es = _split(_bits(_common(topo, _xport(P, r, h), fo)), QH)
+    return [(i, fo[i], es[i]) for i in range(QH)]
+
+
+def _assist(P, topo, o):
+    pl = P["plane_of"][o]
+    own = P["owners"][pl]
+    rest = [r for r in P["planes"][pl] if r not in own]
+    aw = [c for c in [_xport(P, o, h) for h in range(H)] if topo.die(c) != topo.die(P["cores"][o])]
+    if o not in own or not rest or not aw:
+        return None
+    return aw[0], rest[own.index(o) % len(rest)]
+
+
+def _ydests(P, topo, o):
+    a = _assist(P, topo, o)
+    return [d for d in P["planes"][P["plane_of"][o]] if d != o and not (a and d == a[1])]
+
+
+def _idplan(P, topo):
+    cores = P["cores"]
+    send, need = {}, {}
+    for pl, own in enumerate(P["owners"]):
+        lists = []
+        for k in range(Q):
+            h = k // QH
+            lst = [_xport(P, j, h) for j in P["planes"][1 - pl]]
+            lst += [_wport(P, j, h) for j in P["wsrc"] if P["plane_of"][j] != pl]
+            lst += [cores[own[(k - 1) % Q]]]
+            lst += [cores[j] for i, j in enumerate(P["wsrc"]) if P["plane_of"][j] == pl and i % Q == k]
+            lists.append(lst)
+        wf = (128 // max(len(l) for l in lists)) // 8 * 8
+        for k, lst in enumerate(lists):
+            for i, c in enumerate(lst):
+                off = i * wf
+                wid = wf if i < len(lst) - 1 else 128 - off
+                if c in send:
+                    send[c][2].append(cores[own[k]])
+                else:
+                    send[c] = (off, wid, [cores[own[k]]])
+    for c, (off, wid, dests) in send.items():
+        for d in dests:
+            need[d] = need.get(d, 0) + len(_bits(_common(topo, c, dests)))
+    return send, need
 
 
 def _dst(topo, d, src):
@@ -114,27 +173,64 @@ def _col(k):
     return slice(k * CW, (k + 1) * CW)
 
 
-def _helper(g, core, T, topo, P, r):
-    cores = P["cores"]
-    k = [q for q in range(Q) if _port(P, r, q) == core][0]
+def _send_block(g, core, T, topo, P):
+    send, need = _idplan(P, topo)
+    if core not in send:
+        return 0
+    off, wid, dests = send[core]
+    g.vector.memset(T.one[:, 0:wid], 1.0).then_inc(T.sem.fill, 1)
+    g.wait_ge(T.sem.fill, 1)
+    g.affine_select(T.ib[:, 0:wid], T.one[:, 0:wid], [[-1, wid]], AluOpType.is_equal, 0.0, -off, 1).then_inc(T.sem.idb, 1)
+    g.wait_ge(T.sem.idb, 1)
+    m = _common(topo, core, dests)
+    g.remote_dma_fused([RemoteDMATransfer(
+        dst_ids=[_dst(topo, d, core) for d in dests], dma_engine_mask=m, remote_sem=T.sem.ida,
+        srcs=[T.ib[:, 0:wid]], dsts=[T.idn[:, off:off + wid] for d in dests], alu_op=0)], local_sem=T.sem.ls)
+    return len(_bits(m))
+
+
+def _aide_engines(P, topo, o):
+    a = _assist(P, topo, o)
+    c = P["cores"][o]
+    out = _common(topo, c, [P["cores"][d] for d in _ydests(P, topo, o)])
+    return [b for b in _bits(topo.mask(c, a[0])) if not (out >> b) & 1]
+
+
+def _xhelper(g, core, T, topo, P, r, h):
+    xp = [_xport(P, r, i) for i in range(H)]
+    sent = _send_block(g, core, T, topo, P)
+    g.wait_ge(T.sem.hxs, len(_split(_bits(_common(topo, P["cores"][r], xp)), H)[h]))
+    cr = _cross(P, topo, r, h)
+    g.remote_dma_fused([RemoteDMATransfer(
+        dst_ids=[_dst(topo, d, core)], dma_engine_mask=_m(e), remote_sem=T.sem["xa%d" % r],
+        src=T.hx[:, _col(i)], dst=T.xin[:, _col(r)]) for i, d, e in cr], local_sem=T.sem.ls)
+    sent += sum(len(e) for i, d, e in cr)
+    a = _assist(P, topo, r)
+    if a and a[0] == core:
+        k = P["owners"][P["plane_of"][r]].index(r)
+        d = P["cores"][a[1]]
+        m = topo.mask(core, d)
+        rid, pid = topo.addr(d, core)
+        g.wait_ge(T.sem.yh, len(_aide_engines(P, topo, r)))
+        g.remote_dma(out_ap=T.ybuf[:, _col(k)], in_ap=T.hy[:, :], remote_sem=T.sem.ya, local_sem=T.sem.ls,
+                     pid=pid, routing_id=rid, dma_engine_mask=m)
+        sent += len(_bits(m))
+    g.wait_ge(T.sem.ls, sent)
+
+
+def _whelper(g, core, T, topo, P, r, h):
+    gi = P["wsrc"].index(r)
     pl = P["plane_of"][r]
-    far, near = cores[P["owners"][1 - pl][k]], cores[P["owners"][pl][k]]
-    sent = 0
-    if r in P["wsrc"]:
-        gi = P["wsrc"].index(r)
-        dests = [far, near]
+    wp = [_wport(P, r, i) for i in range(H)]
+    sent = _send_block(g, core, T, topo, P)
+    g.wait_ge(T.sem.hw, len(_bits(_common(topo, P["cores"][r], wp))))
+    for p in (1 - pl, pl):
+        dests = _pair(P, p, h)
         m = _common(topo, core, dests)
-        g.wait_ge(T.sem.hw, len(_bits(_common(topo, cores[r], P["ports"][r]))))
         g.remote_dma_fused([RemoteDMATransfer(
             dst_ids=[_dst(topo, d, core) for d in dests], dma_engine_mask=m, remote_sem=T.sem.wa,
             srcs=[T.wd[:, :]], dsts=[T.wb[:, gi * 128:(gi + 1) * 128] for d in dests], alu_op=0)], local_sem=T.sem.ls)
         sent += len(_bits(m))
-    g.wait_ge(T.sem.hxs, len(_split(_bits(_common(topo, cores[r], P["ports"][r])), Q)[k]))
-    m = topo.mask(core, far)
-    rid, pid = topo.addr(far, core)
-    g.remote_dma(out_ap=T.xin[:, _col(r)], in_ap=T.hx[:, :], remote_sem=T.sem.xc, local_sem=T.sem.ls,
-                 pid=pid, routing_id=rid, dma_engine_mask=m)
-    sent += len(_bits(m))
     g.wait_ge(T.sem.ls, sent)
 
 
@@ -144,12 +240,14 @@ def rank_program(g, core, T, topo):
     rank = T.rank_of(core)
     if rank is None:
         for r in range(n):
-            if core in P["ports"][r]:
-                _helper(g, core, T, topo, P, r)
+            for h in range(H):
+                if core == _xport(P, r, h):
+                    _xhelper(g, core, T, topo, P, r, h)
+                elif r in P["wsrc"] and core == _wport(P, r, h):
+                    _whelper(g, core, T, topo, P, r, h)
         return
 
     pl = P["plane_of"][rank]
-    plane = P["planes"][pl]
     own = P["owners"][pl]
     is_owner = rank in own
     sent = 0
@@ -157,79 +255,78 @@ def rank_program(g, core, T, topo):
     g.sync.dma_start(T.xs[:, :], T.x[:, :]).then_inc(T.sem.xl, 16)
     if rank in P["wsrc"]:
         g.scalar.dma_start(T.wd[:, :], T.w[:, :]).then_inc(T.sem.wl, 16)
+    sent += _send_block(g, core, T, topo, P)
     if is_owner:
-        g.vector.memset(T.ida[:, 0:1], 1.0).then_inc(T.sem.fill, 1)
-        g.vector.memset(T.ida[:, 1:129], 0.0).then_inc(T.sem.fill, 1)
-        g.vector.memset(T.zero[:, :], 0.0).then_inc(T.sem.fill, 1)
-        g.scalar.wait_ge(T.sem.fill, 3)
-        g.scalar.dma_start(T.idd[:, :], T.ida[:, :]).then_inc(T.sem.id1, 16)
-        g.scalar.wait_ge(T.sem.id1, 16)
-        g.scalar.dma_start(T.idn[:, :], T.idd[0:128, :]).then_inc(T.sem.id2, 16)
+        g.vector.memset(T.zero[:, :], 0.0).then_inc(T.sem.fz, 1)
 
-    pc = P["ports"][rank]
-    chipmask = _common(topo, core, pc)
     if rank in P["wsrc"]:
+        wp = [_wport(P, rank, h) for h in range(H)]
+        wm = _common(topo, core, wp)
         g.wait_ge(T.sem.wl, 16)
         g.remote_dma_fused([RemoteDMATransfer(
-            dst_ids=[_dst(topo, c, core) for c in pc], dma_engine_mask=chipmask, remote_sem=T.sem.hw,
-            srcs=[T.wd[:, :]], dsts=[T.wd[:, :] for c in pc], alu_op=0)], local_sem=T.sem.ls)
-        sent += len(_bits(chipmask))
+            dst_ids=[_dst(topo, c, core) for c in wp], dma_engine_mask=wm, remote_sem=T.sem.hw,
+            srcs=[T.wd[:, :]], dsts=[T.wd[:, :] for c in wp], alu_op=0)], local_sem=T.sem.ls)
+        sent += len(_bits(wm))
 
     g.wait_ge(T.sem.xl, 16)
-    eng = _split(_bits(chipmask), Q)
+    xp = [_xport(P, rank, h) for h in range(H)]
+    eng = _split(_bits(_common(topo, core, xp)), H)
     g.remote_dma_fused([RemoteDMATransfer(
-        dst_ids=[_dst(topo, _port(P, rank, k), core)], dma_engine_mask=_m(eng[k]), remote_sem=T.sem.hxs,
-        src=T.xs[:, _col(k)], dst=T.hx[:, :]) for k in range(Q)], local_sem=T.sem.ls)
+        dst_ids=[_dst(topo, xp[h], core)], dma_engine_mask=_m(eng[h]), remote_sem=T.sem.hxs,
+        src=T.xs[:, h * QH * CW:(h + 1) * QH * CW], dst=T.hx[:, :]) for h in range(H)], local_sem=T.sem.ls)
     sent += sum(len(e) for e in eng)
     dr = _direct(P, topo, rank)
     g.remote_dma_fused([RemoteDMATransfer(
-        dst_ids=[_dst(topo, cores[o], core)], dma_engine_mask=_m(e), remote_sem=T.sem.xd,
+        dst_ids=[_dst(topo, cores[o], core)], dma_engine_mask=_m(e), remote_sem=T.sem["xa%d" % rank],
         src=T.xs[:, _col(k)], dst=T.xin[:, _col(rank)]) for k, o, e in dr], local_sem=T.sem.ls)
     sent += sum(len(e) for k, o, e in dr)
 
     n_y = 0
     for o in own:
         if o != rank:
-            n_y += len(_bits(_common(topo, cores[o], [cores[d] for d in plane if d != o])))
+            a = _assist(P, topo, o)
+            if a and a[1] == rank:
+                n_y += len(_bits(topo.mask(a[0], core)))
+            else:
+                n_y += len(_bits(_common(topo, cores[o], [cores[d] for d in _ydests(P, topo, o)])))
 
     if is_owner:
         k = own.index(rank)
-        n_xd = sum(len(e) for j in plane if j != rank for q, o, e in _direct(P, topo, j) if o == rank)
-        far = [j for j in range(n) if P["plane_of"][j] != pl]
-        n_xc = sum(len(_bits(topo.mask(_port(P, j, k), core))) for j in far)
-        n_wa = sum(len(_bits(_common(topo, _port(P, j, k), [core]))) for j in P["wsrc"])
+        cnt = {}
+        for j in range(n):
+            if j == rank:
+                continue
+            if P["plane_of"][j] == pl:
+                cnt[j] = sum(len(e) for q, o, e in _direct(P, topo, j) if o == rank)
+            else:
+                cnt[j] = sum(len(e) for i, d, e in _cross(P, topo, j, k // QH) if d == core)
+        n_wa = sum(len(_bits(_common(topo, _wport(P, j, k // QH), _pair(P, pl, k // QH)))) for j in P["wsrc"])
+        n_ida = _idplan(P, topo)[1][core]
         ps = [T.ps0, T.ps1]
         tt = [T.t0, T.t1]
         sm = [T.sem.sm0, T.sem.sm1]
         ts = [T.sem.ts0, T.sem.ts1]
-        te, ve = g.tensor, g.vector
+        te, ve, se = g.tensor, g.vector, g.scalar
 
-        def add(gi, j):
-            seq = _order(P, gi, rank)
+        seq = _order(P, rank, cnt)
+        te.wait_ge(T.sem.ida, n_ida)
+        te.wait_ge(T.sem.xl, 16)
+        for j in seq:
+            gi = [i for i, grp in enumerate(P["groups"]) if j in grp][0]
+            mine = [i for i in seq if i in P["groups"][gi]]
+            if j != rank:
+                te.wait_ge(T.sem["xa%d" % j], cnt[j])
             rhs = T.xs[:, _col(k)] if j == rank else T.xin[:, _col(j)]
-            ins = te.matmul(ps[gi][:, 0:CW], T.idn[:, :], rhs, j == seq[0], j == seq[-1])
-            if j == seq[-1]:
+            ins = te.matmul(ps[gi][:, 0:CW], T.idn[:, :], rhs, j == mine[0], j == mine[-1])
+            if j == mine[-1]:
                 ins.then_inc(sm[gi], 1)
 
-        te.wait_ge(T.sem.id2, 16)
-        te.wait_ge(T.sem.xl, 16)
-        for gi, grp in enumerate(P["groups"]):
-            if rank in grp:
-                add(gi, rank)
-        te.wait_ge(T.sem.xd, n_xd)
-        for gi, grp in enumerate(P["groups"]):
-            for j in _order(P, gi, rank):
-                if j != rank and P["plane_of"][j] == pl:
-                    add(gi, j)
-        te.wait_ge(T.sem.xc, n_xc)
-        for gi, grp in enumerate(P["groups"]):
-            for j in _order(P, gi, rank):
-                if P["plane_of"][j] != pl:
-                    add(gi, j)
-        ve.wait_ge(T.sem.fill, 3)
-        for gi in range(len(ps)):
-            ve.wait_ge(sm[gi], 1)
-            ve.tensor_tensor(tt[gi][:, :], ps[gi][:, 0:CW], T.zero[:, :], AluOpType.max).then_inc(ts[gi], 1)
+        ve.wait_ge(T.sem.fz, 1)
+        ve.wait_ge(sm[0], 1)
+        ve.tensor_tensor(tt[0][:, :], ps[0][:, 0:CW], T.zero[:, :], AluOpType.max).then_inc(ts[0], 1)
+        se.wait_ge(sm[1], 1)
+        se.activation(tt[1][:, :], ps[1][:, 0:CW], ActivationFunctionType.Relu).then_inc(ts[1], 1)
+
         te.wait_ge(T.sem.wa, n_wa)
         for gi in range(len(ps)):
             te.wait_ge(ts[gi], 1)
@@ -238,13 +335,21 @@ def rank_program(g, core, T, topo):
         ve.wait_ge(T.sem.ys, 1)
         ve.tensor_copy(T.ybuf[:, _col(k)], T.psy[:, 0:CW]).then_inc(T.sem.yc, 1)
 
-        dests = [cores[d] for d in plane if d != rank]
+        dests = [cores[d] for d in _ydests(P, topo, rank)]
         m = _common(topo, core, dests)
-        g.wait_ge(T.sem.yc, 1)
-        g.remote_dma_fused([RemoteDMATransfer(
+        tr = [RemoteDMATransfer(
             dst_ids=[_dst(topo, d, core) for d in dests], dma_engine_mask=m, remote_sem=T.sem.ya,
-            srcs=[T.ybuf[:, _col(k)]], dsts=[T.ybuf[:, _col(k)] for d in dests], alu_op=0)], local_sem=T.sem.ls)
+            srcs=[T.ybuf[:, _col(k)]], dsts=[T.ybuf[:, _col(k)] for d in dests], alu_op=0)]
         sent += len(_bits(m))
+        a = _assist(P, topo, rank)
+        if a:
+            ae = _aide_engines(P, topo, rank)
+            tr.append(RemoteDMATransfer(
+                dst_ids=[_dst(topo, a[0], core)], dma_engine_mask=_m(ae), remote_sem=T.sem.yh,
+                src=T.ybuf[:, _col(k)], dst=T.hy[:, :]))
+            sent += len(ae)
+        g.wait_ge(T.sem.yc, 1)
+        g.remote_dma_fused(tr, local_sem=T.sem.ls)
         g.sync.wait_ge(T.sem.yc, 1)
 
     g.sync.wait_ge(T.sem.ya, n_y)
@@ -253,8 +358,11 @@ def rank_program(g, core, T, topo):
     g.wait_ge(T.sem.ls, sent)
 
 
-def _order(P, gi, rank):
+def _order(P, rank, cnt):
     pl = P["plane_of"][rank]
-    grp = P["groups"][gi]
-    return ([j for j in grp if j == rank] + [j for j in grp if j != rank and P["plane_of"][j] == pl]
-            + [j for j in grp if P["plane_of"][j] != pl])
+    w = P["wsrc"]
+    far = [j for j in range(P["n"]) if P["plane_of"][j] != pl]
+    near = [j for j in range(P["n"]) if P["plane_of"][j] == pl and j != rank]
+    near_n = sorted([j for j in near if j not in w], key=lambda j: -cnt[j])
+    return ([rank] + [j for j in far if j not in w] + [j for j in far if j in w]
+            + near_n + [j for j in near if j in w])

import comms_topo
from concourse.bass import DstId, RemoteDMATransfer
from concourse.mybir import dt, AluOpType, ActivationFunctionType

Q = 4
CW = 128
H = 2
QH = Q // H

SCRATCH = {
    "xs": ("sbuf", [128, 512], "bfloat16"),
    "xin": ("sbuf", [128, 10 * CW], "bfloat16"),
    "hx": ("sbuf", [128, QH * CW], "bfloat16"),
    "hy": ("sbuf", [128, CW], "bfloat16"),
    "wd": ("dram", [128, 128], "bfloat16"),
    "wb": ("sbuf", [128, 2 * 128], "bfloat16"),
    "ybuf": ("sbuf", [128, 512], "bfloat16"),
    "one": ("sbuf", [128, 128], "bfloat16"),
    "ib": ("sbuf", [128, 128], "bfloat16"),
    "idn": ("sbuf", [128, 128], "bfloat16"),
    "zero": ("sbuf", [128, CW], "float32"),
    "t0": ("sbuf", [128, CW], "bfloat16"),
    "t1": ("sbuf", [128, CW], "bfloat16"),
    "ps0": ("psum", [128, 512], "float32"),
    "ps1": ("psum", [128, 512], "float32"),
    "psy": ("psum", [128, 512], "float32"),
}
SEMAPHORES = ["xl", "wl", "hw", "hxs", "wa", "ya", "yh", "ls", "fill", "fz", "idb", "ida",
              "sm0", "sm1", "ts0", "ts1", "ys", "yc", "st"] + ["xa%d" % j for j in range(10)]


def _bits(mask):
    return [b for b in range(mask.bit_length()) if (mask >> b) & 1]


def _m(bits):
    return sum(1 << b for b in bits)


def _split(bits, n):
    p = 1
    while p * 2 * n <= len(bits):
        p *= 2
    sizes = [p] * n
    left = len(bits) - p * n
    for i in range(n):
        if left >= sizes[i]:
            left -= sizes[i]
            sizes[i] *= 2
    out, o = [], 0
    for s in sizes:
        out.append(bits[o:o + s])
        o += s
    return out


def _plan(T, topo):
    cores = list(T.cores)
    n = len(cores)
    groups = T.tables["GROUPS"]
    wsrc = [grp[0] for grp in groups]
    planes = []
    for r in range(n):
        for p in planes:
            if topo.same_plane(cores[r], cores[p[0]]):
                p.append(r)
                break
        else:
            planes.append([r])
    plane_of = {}
    for i, p in enumerate(planes):
        for r in p:
            plane_of[r] = i
    owners = [[r for r in p if r not in wsrc][:Q] for p in planes]
    hosts = 1 + max(topo.host(c) for c in cores)
    ports = {}
    for r in range(n):
        rc = cores[r]
        far = cores[planes[1 - plane_of[r]][0]]
        can = [c for c in range(hosts * topo.CORES_PER_HOST)
               if c != rc and topo.host(c) == topo.host(rc) and topo.chip(c) == topo.chip(rc) and topo.may_write(c, far)]
        near = [c for c in can if topo.die(c) == topo.die(rc)]
        away = [c for c in can if topo.die(c) != topo.die(rc)]
        order = []
        for a, b in zip(near, away):
            order += [a, b]
        ports[r] = order[:2 * H]
    return {"cores": cores, "n": n, "groups": groups, "wsrc": wsrc, "planes": planes, "plane_of": plane_of,
            "owners": owners, "ports": ports}


def _xport(P, r, h):
    return P["ports"][r][(h + P["planes"][P["plane_of"][r]].index(r)) % H]


def _wport(P, r, h):
    return P["ports"][r][H + (h + P["wsrc"].index(r)) % H]


def _pair(P, pl, h):
    return [P["cores"][P["owners"][pl][h * QH + i]] for i in range(QH)]


def _direct(P, topo, r):
    own = P["owners"][P["plane_of"][r]]
    todo = [(k, o) for k, o in enumerate(own) if o != r]
    src = P["cores"][r]
    bits = _bits(topo.mask(src, P["cores"][todo[0][1]]))
    return [(k, o, e) for (k, o), e in zip(todo, _split(bits, len(todo)))]


def _cross(P, topo, r, h):
    fo = _pair(P, 1 - P["plane_of"][r], h)
    es = _split(_bits(_common(topo, _xport(P, r, h), fo)), QH)
    return [(i, fo[i], es[i]) for i in range(QH)]


def _assist(P, topo, o):
    pl = P["plane_of"][o]
    own = P["owners"][pl]
    rest = [r for r in P["planes"][pl] if r not in own]
    aw = [c for c in [_xport(P, o, h) for h in range(H)] if topo.die(c) != topo.die(P["cores"][o])]
    if o not in own or not rest or not aw:
        return None
    return aw[0], rest[own.index(o) % len(rest)]


def _ydests(P, topo, o):
    a = _assist(P, topo, o)
    return [d for d in P["planes"][P["plane_of"][o]] if d != o and not (a and d == a[1])]


def _idplan(P, topo):
    cores = P["cores"]
    send, need = {}, {}
    for pl, own in enumerate(P["owners"]):
        lists = []
        for k in range(Q):
            h = k // QH
            lst = [_xport(P, j, h) for j in P["planes"][1 - pl]]
            lst += [_wport(P, j, h) for j in P["wsrc"] if P["plane_of"][j] != pl]
            lst += [cores[own[(k - 1) % Q]]]
            lst += [cores[j] for i, j in enumerate(P["wsrc"]) if P["plane_of"][j] == pl and i % Q == k]
            lists.append(lst)
        wf = (128 // max(len(l) for l in lists)) // 8 * 8
        for k, lst in enumerate(lists):
            for i, c in enumerate(lst):
                off = i * wf
                wid = wf if i < len(lst) - 1 else 128 - off
                if c in send:
                    send[c][2].append(cores[own[k]])
                else:
                    send[c] = (off, wid, [cores[own[k]]])
    for c, (off, wid, dests) in send.items():
        for d in dests:
            need[d] = need.get(d, 0) + len(_bits(_common(topo, c, dests)))
    return send, need


def _dst(topo, d, src):
    rid, pid = topo.addr(d, src)
    return DstId(rid=rid, pnc=pid)


def _common(topo, src, dests):
    m = topo.mask(src, dests[0])
    for d in dests[1:]:
        m &= topo.mask(src, d)
    return m


def _col(k):
    return slice(k * CW, (k + 1) * CW)


def _send_block(g, core, T, topo, P):
    send, need = _idplan(P, topo)
    if core not in send:
        return 0
    off, wid, dests = send[core]
    g.vector.memset(T.one[:, 0:wid], 1.0).then_inc(T.sem.fill, 1)
    g.wait_ge(T.sem.fill, 1)
    g.affine_select(T.ib[:, 0:wid], T.one[:, 0:wid], [[-1, wid]], AluOpType.is_equal, 0.0, -off, 1).then_inc(T.sem.idb, 1)
    g.wait_ge(T.sem.idb, 1)
    m = _common(topo, core, dests)
    g.remote_dma_fused([RemoteDMATransfer(
        dst_ids=[_dst(topo, d, core) for d in dests], dma_engine_mask=m, remote_sem=T.sem.ida,
        srcs=[T.ib[:, 0:wid]], dsts=[T.idn[:, off:off + wid] for d in dests], alu_op=0)], local_sem=T.sem.ls)
    return len(_bits(m))


def _aide_engines(P, topo, o):
    a = _assist(P, topo, o)
    c = P["cores"][o]
    out = _common(topo, c, [P["cores"][d] for d in _ydests(P, topo, o)])
    return [b for b in _bits(topo.mask(c, a[0])) if not (out >> b) & 1]


def _xhelper(g, core, T, topo, P, r, h):
    xp = [_xport(P, r, i) for i in range(H)]
    sent = _send_block(g, core, T, topo, P)
    g.wait_ge(T.sem.hxs, len(_split(_bits(_common(topo, P["cores"][r], xp)), H)[h]))
    cr = _cross(P, topo, r, h)
    g.remote_dma_fused([RemoteDMATransfer(
        dst_ids=[_dst(topo, d, core)], dma_engine_mask=_m(e), remote_sem=T.sem["xa%d" % r],
        src=T.hx[:, _col(i)], dst=T.xin[:, _col(r)]) for i, d, e in cr], local_sem=T.sem.ls)
    sent += sum(len(e) for i, d, e in cr)
    a = _assist(P, topo, r)
    if a and a[0] == core:
        k = P["owners"][P["plane_of"][r]].index(r)
        d = P["cores"][a[1]]
        m = topo.mask(core, d)
        rid, pid = topo.addr(d, core)
        g.wait_ge(T.sem.yh, len(_aide_engines(P, topo, r)))
        g.remote_dma(out_ap=T.ybuf[:, _col(k)], in_ap=T.hy[:, :], remote_sem=T.sem.ya, local_sem=T.sem.ls,
                     pid=pid, routing_id=rid, dma_engine_mask=m)
        sent += len(_bits(m))
    g.wait_ge(T.sem.ls, sent)


def _whelper(g, core, T, topo, P, r, h):
    gi = P["wsrc"].index(r)
    pl = P["plane_of"][r]
    wp = [_wport(P, r, i) for i in range(H)]
    sent = _send_block(g, core, T, topo, P)
    g.wait_ge(T.sem.hw, len(_bits(_common(topo, P["cores"][r], wp))))
    for p in (1 - pl, pl):
        dests = _pair(P, p, h)
        m = _common(topo, core, dests)
        g.remote_dma_fused([RemoteDMATransfer(
            dst_ids=[_dst(topo, d, core) for d in dests], dma_engine_mask=m, remote_sem=T.sem.wa,
            srcs=[T.wd[:, :]], dsts=[T.wb[:, gi * 128:(gi + 1) * 128] for d in dests], alu_op=0)], local_sem=T.sem.ls)
        sent += len(_bits(m))
    g.wait_ge(T.sem.ls, sent)


def rank_program(g, core, T, topo):
    P = _plan(T, topo)
    cores, n = P["cores"], P["n"]
    rank = T.rank_of(core)
    if rank is None:
        for r in range(n):
            for h in range(H):
                if core == _xport(P, r, h):
                    _xhelper(g, core, T, topo, P, r, h)
                elif r in P["wsrc"] and core == _wport(P, r, h):
                    _whelper(g, core, T, topo, P, r, h)
        return

    pl = P["plane_of"][rank]
    own = P["owners"][pl]
    is_owner = rank in own
    sent = 0

    g.sync.dma_start(T.xs[:, :], T.x[:, :]).then_inc(T.sem.xl, 16)
    if rank in P["wsrc"]:
        g.scalar.dma_start(T.wd[:, :], T.w[:, :]).then_inc(T.sem.wl, 16)
    sent += _send_block(g, core, T, topo, P)
    if is_owner:
        g.vector.memset(T.zero[:, :], 0.0).then_inc(T.sem.fz, 1)

    if rank in P["wsrc"]:
        wp = [_wport(P, rank, h) for h in range(H)]
        wm = _common(topo, core, wp)
        g.wait_ge(T.sem.wl, 16)
        g.remote_dma_fused([RemoteDMATransfer(
            dst_ids=[_dst(topo, c, core) for c in wp], dma_engine_mask=wm, remote_sem=T.sem.hw,
            srcs=[T.wd[:, :]], dsts=[T.wd[:, :] for c in wp], alu_op=0)], local_sem=T.sem.ls)
        sent += len(_bits(wm))

    g.wait_ge(T.sem.xl, 16)
    xp = [_xport(P, rank, h) for h in range(H)]
    eng = _split(_bits(_common(topo, core, xp)), H)
    g.remote_dma_fused([RemoteDMATransfer(
        dst_ids=[_dst(topo, xp[h], core)], dma_engine_mask=_m(eng[h]), remote_sem=T.sem.hxs,
        src=T.xs[:, h * QH * CW:(h + 1) * QH * CW], dst=T.hx[:, :]) for h in range(H)], local_sem=T.sem.ls)
    sent += sum(len(e) for e in eng)
    dr = _direct(P, topo, rank)
    g.remote_dma_fused([RemoteDMATransfer(
        dst_ids=[_dst(topo, cores[o], core)], dma_engine_mask=_m(e), remote_sem=T.sem["xa%d" % rank],
        src=T.xs[:, _col(k)], dst=T.xin[:, _col(rank)]) for k, o, e in dr], local_sem=T.sem.ls)
    sent += sum(len(e) for k, o, e in dr)

    n_y = 0
    for o in own:
        if o != rank:
            a = _assist(P, topo, o)
            if a and a[1] == rank:
                n_y += len(_bits(topo.mask(a[0], core)))
            else:
                n_y += len(_bits(_common(topo, cores[o], [cores[d] for d in _ydests(P, topo, o)])))

    if is_owner:
        k = own.index(rank)
        cnt = {}
        for j in range(n):
            if j == rank:
                continue
            if P["plane_of"][j] == pl:
                cnt[j] = sum(len(e) for q, o, e in _direct(P, topo, j) if o == rank)
            else:
                cnt[j] = sum(len(e) for i, d, e in _cross(P, topo, j, k // QH) if d == core)
        n_wa = sum(len(_bits(_common(topo, _wport(P, j, k // QH), _pair(P, pl, k // QH)))) for j in P["wsrc"])
        n_ida = _idplan(P, topo)[1][core]
        ps = [T.ps0, T.ps1]
        tt = [T.t0, T.t1]
        sm = [T.sem.sm0, T.sem.sm1]
        ts = [T.sem.ts0, T.sem.ts1]
        te, ve, se = g.tensor, g.vector, g.scalar

        seq = _order(P, rank, cnt)
        te.wait_ge(T.sem.ida, n_ida)
        te.wait_ge(T.sem.xl, 16)
        for j in seq:
            gi = [i for i, grp in enumerate(P["groups"]) if j in grp][0]
            mine = [i for i in seq if i in P["groups"][gi]]
            if j != rank:
                te.wait_ge(T.sem["xa%d" % j], cnt[j])
            rhs = T.xs[:, _col(k)] if j == rank else T.xin[:, _col(j)]
            ins = te.matmul(ps[gi][:, 0:CW], T.idn[:, :], rhs, j == mine[0], j == mine[-1])
            if j == mine[-1]:
                ins.then_inc(sm[gi], 1)

        ve.wait_ge(T.sem.fz, 1)
        ve.wait_ge(sm[0], 1)
        ve.tensor_tensor(tt[0][:, :], ps[0][:, 0:CW], T.zero[:, :], AluOpType.max).then_inc(ts[0], 1)
        se.wait_ge(sm[1], 1)
        se.activation(tt[1][:, :], ps[1][:, 0:CW], ActivationFunctionType.Relu).then_inc(ts[1], 1)

        te.wait_ge(T.sem.wa, n_wa)
        for gi in range(len(ps)):
            te.wait_ge(ts[gi], 1)
            ins = te.matmul(T.psy[:, 0:CW], T.wb[:, gi * 128:(gi + 1) * 128], tt[gi][:, :], gi == 0, gi == len(ps) - 1)
        ins.then_inc(T.sem.ys, 1)
        ve.wait_ge(T.sem.ys, 1)
        ve.tensor_copy(T.ybuf[:, _col(k)], T.psy[:, 0:CW]).then_inc(T.sem.yc, 1)

        dests = [cores[d] for d in _ydests(P, topo, rank)]
        m = _common(topo, core, dests)
        tr = [RemoteDMATransfer(
            dst_ids=[_dst(topo, d, core) for d in dests], dma_engine_mask=m, remote_sem=T.sem.ya,
            srcs=[T.ybuf[:, _col(k)]], dsts=[T.ybuf[:, _col(k)] for d in dests], alu_op=0)]
        sent += len(_bits(m))
        a = _assist(P, topo, rank)
        if a:
            ae = _aide_engines(P, topo, rank)
            tr.append(RemoteDMATransfer(
                dst_ids=[_dst(topo, a[0], core)], dma_engine_mask=_m(ae), remote_sem=T.sem.yh,
                src=T.ybuf[:, _col(k)], dst=T.hy[:, :]))
            sent += len(ae)
        g.wait_ge(T.sem.yc, 1)
        g.remote_dma_fused(tr, local_sem=T.sem.ls)
        g.sync.wait_ge(T.sem.yc, 1)

    g.sync.wait_ge(T.sem.ya, n_y)
    g.sync.dma_start(T.y[:, :], T.ybuf[:, :]).then_inc(T.sem.st, 16)
    g.sync.wait_ge(T.sem.st, 16)
    g.wait_ge(T.sem.ls, sent)


def _order(P, rank, cnt):
    pl = P["plane_of"][rank]
    w = P["wsrc"]
    far = [j for j in range(P["n"]) if P["plane_of"][j] != pl]
    near = [j for j in range(P["n"]) if P["plane_of"][j] == pl and j != rank]
    near_n = sorted([j for j in near if j not in w], key=lambda j: -cnt[j])
    return ([rank] + [j for j in far if j not in w] + [j for j in far if j in w]
            + near_n + [j for j in near if j in w])
